import numpy as np
import ml_dtypes


def mxq(x, axis, fmt="e4m3"):
    dtype, down = {"e4m3": (ml_dtypes.float8_e4m3fn, 7), "e5m2": (ml_dtypes.float8_e5m2, 14)}[fmt]
    v = np.moveaxis(np.asarray(x, np.float32).astype(ml_dtypes.bfloat16).astype(np.float64), axis, -1)
    blocks = v.reshape(v.shape[:-1] + (-1, 32))
    amax = np.abs(blocks).max(-1, keepdims=True)
    byte = np.maximum(np.where(amax > 0, np.frexp(amax)[1] - 1 + 127, 0) - down, 1)
    scale = np.exp2(byte - 127.0)
    codes = (blocks / scale).astype(np.float32).astype(dtype).astype(np.float64)
    return np.moveaxis((codes * scale).reshape(v.shape), -1, axis)


WIDE = False


def mx_kscale(k):
    if not WIDE:
        return np.ones(k)
    levels = np.array([10, -10, 5, -5, 0])
    if k % 512:
        return np.exp2(np.random.permutation(np.resize(levels, k // 32))).repeat(32)
    a = np.empty((k // 512, 16))
    for p in range(k // 512):
        a[p, :8] = np.random.permutation(np.resize(levels, 8))
        for g in range(8):
            far = levels[np.abs(levels - a[p, g]) >= 10]
            a[p, g + 8] = far[np.random.randint(len(far))]
    return np.exp2(a.ravel()).repeat(32)


def f64(x):
    return np.asarray(x).astype(np.float64)


def striped(idx):
    return np.tile(idx.reshape(-1, 16).T, (8, 1)).astype(np.uint16)


def unstriped(offs):
    return offs[:16].T.reshape(-1).astype(np.int64)


def pack_weight(w):
    k, n = w.shape
    w = f64(np.asarray(w, np.float32).astype(ml_dtypes.bfloat16)).reshape(k // 32, 32, n)
    amax = np.abs(w).max(1)
    byte = np.clip(np.where(amax > 0, np.frexp(amax)[1] - 1 + 127 - 7, 1), 1, 254)
    scaled = (w * np.exp2(127.0 - byte)[:, None, :]).reshape(k, n).astype(np.float32)
    words = np.ascontiguousarray(scaled.reshape(k // 512, 128, 4, n).transpose(0, 1, 3, 2)).astype(ml_dtypes.float8_e4m3fn).view(np.uint8)
    return words, np.ascontiguousarray(byte.astype(np.uint8).reshape(k // 512, 16, n))


def unpack_weight(words, scales):
    g, p, n, _ = words.shape
    vals = np.ascontiguousarray(words).view(ml_dtypes.float8_e4m3fn).astype(np.float64) * np.repeat(np.exp2(scales.astype(np.float64) - 127.0), 8, axis=1)[..., None]
    return vals.transpose(0, 1, 3, 2).reshape(g * 512, n)


K, T, S, D, N, H, V, U = 1024, 2048, 1024, 4, 128, 512, 256, 512


def setup_inputs():
    n = np.random.standard_normal
    s = mx_kscale(K)[:, None]
    u = mx_kscale(H)
    packed_xT = pack_weight(n((K, T)) * s)
    return {
        "x_words": packed_xT[0],
        "x_scales": packed_xT[1],
        "w1": (n((K, H)) / np.sqrt(K) / s).astype(np.float32),
        "w2": (n((K, H)) / np.sqrt(K) / s).astype(np.float32),
        "qry": (n((H, U))).astype(np.float32),
        "unit": (np.random.uniform(0.6, 1.4, (H, 1)) * u[:, None]).astype(np.float32),
        "w3": (n((H, N)) / np.sqrt(H) / u[:, None]).astype(np.float32),
        "offs": striped(np.random.permutation(T)[:S]),
        "b1": striped(np.random.permutation(np.concatenate([np.arange(V), np.random.randint(0, V, U - V)]))),
        "b2": striped(np.random.permutation(np.concatenate([np.arange(V), np.random.randint(0, V, U - V)]))),
        "b3": striped(np.random.permutation(np.concatenate([np.arange(V), np.random.randint(0, V, U - V)]))),
    }


def reference(x_words, x_scales, w1, w2, qry, unit, w3, offs, b1, b2, b3):
    xq = unpack_weight(x_words, x_scales)[:, unstriped(offs)]
    y = mxq(f64(w1), 0, "e4m3").T @ xq
    blk = y.reshape(len(y), -1, D).mean(axis=2)
    e1 = np.exp(np.tanh(blk[:, unstriped(b1)] * f64(qry)))
    yv = mxq(f64(w2), 0, "e4m3").T @ xq
    vblk = yv.reshape(len(yv), -1, D).mean(axis=2)
    e2 = np.exp(np.tanh(blk[:, unstriped(b2)] * f64(qry)))
    e3 = np.exp(np.tanh(blk[:, unstriped(b3)] * f64(qry)))
    num = e1 * vblk[:, unstriped(b1)] + e2 * vblk[:, unstriped(b2)] + e3 * vblk[:, unstriped(b3)]
    den = e1 + e2 + e3
    hid = f64(unit) * (num / den)
    return mxq(f64(w3), 0, "e4m3").T @ mxq(hid, 0, "e4m3")

@@ -1,0 +1,244 @@
+from contextlib import ExitStack
+
+import concourse.mybir as mybir
+from concourse.masks import make_identity
+
+K, T, S, D, N, H, V, U = 1024, 2048, 1024, 4, 128, 512, 256, 512
+FLOPS = 2 * (2 * K * H * S + H * N * U)
+
+F32 = mybir.dt.float32
+BF16 = mybir.dt.bfloat16
+I32 = mybir.dt.int32
+U32 = mybir.dt.uint32
+U16 = mybir.dt.uint16
+U8 = mybir.dt.uint8
+FP8X4 = mybir.dt.float8_e4m3fn_x4
+ACT = mybir.ActivationFunctionType
+MULT = mybir.AluOpType.mult
+
+P = 128
+PACK = 4
+PASSES = K // (P * PACK)
+TILES = H // P
+LISTS = 3
+WCOLS = 256
+HALF = U // 2
+KEY_WINDOW = U + 16
+VAL_WINDOW = HALF + 16
+
+
+def tile_picked_ymoba_avg_p_kernel(tc, x_words, x_scales, w1, w2, qry, unit, w3, offs, b1, b2, b3, out):
+    nc = tc.nc
+    with ExitStack() as ctx:
+        keep = ctx.enter_context(tc.tile_pool(name="keep", bufs=1))
+        psum = ctx.enter_context(tc.psum_pool(name="psum", bufs=1))
+
+        def bank(b, shape, name):
+            return psum.tile(shape, F32, name=name, tag="bank%d" % b)
+
+        offs_t = keep.tile([P, S // 16], U16, name="offs_t")
+        lists = [keep.tile([P, U // 16], U16, name="list%d" % l) for l in range(LISTS)]
+        xw = [keep.tile([P, T], U32, name="xw%d" % o, align_bytes=64) for o in range(PASSES)]
+        xs = keep.tile([P, T], U8, name="xs", align_bytes=64)
+        ident = keep.tile([P, P], F32, name="ident")
+        kwin = {}
+        vwin = [keep.tile([P, VAL_WINDOW], F32, name="vwin%d" % t, align_bytes=64) for t in range(TILES)]
+        q = [keep.tile([P, U], F32, name="q%d" % t, tag="q%d" % t, align_bytes=64) for t in range(TILES)]
+        unit_t = keep.tile([P, TILES], F32, name="unit_t")
+        wraw = {}
+        for m in range(2):
+            for o in range(PASSES):
+                for c in range(2):
+                    wraw[m, o, c] = keep.tile([P, PACK, WCOLS], F32, name="wraw%d%d%d" % (m, o, c), tag=({(1, 0, 0): "kwin1", (1, 1, 0): "kwin2", (1, 0, 1): "kwin3", (1, 1, 1): "bounded"}.get((m, o, c), "wraw%d%d%d" % (m, o, c))), align_bytes=64)
+        w3raw = keep.tile([P, PACK, N], F32, name="w3raw", align_bytes=64)
+
+        nc.gpsimd.memset(xs[:].bitcast(I32), 0)
+
+        def load_w(m, o, c):
+            w = (w1, w2)[m]
+            rows = w[o * P * PACK : (o + 1) * P * PACK, c * WCOLS : (c + 1) * WCOLS]
+            nc.sync.dma_start(out=wraw[m, o, c][:], in_=rows.rearrange("(p j) c -> p j c", j=PACK))
+
+        def load_x(o):
+            nc.sync.dma_start(out=xw[o][:].bitcast(I32), in_=x_words[o].rearrange("p n t -> p (n t)").bitcast(I32))
+
+        def load_q(t):
+            nc.sync.dma_start(out=q[t][:], in_=qry[t * P : (t + 1) * P, :])
+
+        nc.sync.dma_start(offs_t[:], offs)
+        load_w(0, 0, 0)
+        for quad in range(4):
+            nc.sync.dma_start(out=xs[32 * quad : 32 * quad + 8, :].bitcast(I32), in_=x_scales[:, 4 * quad : 4 * quad + 4, :].bitcast(I32))
+        load_x(0)
+        load_x(1)
+        load_w(0, 1, 0)
+        nc.sync.dma_start(lists[0][:], b1)
+        load_q(0)
+        nc.sync.dma_start(lists[1][:], b2)
+        nc.sync.dma_start(lists[2][:], b3)
+        load_w(0, 0, 1)
+        load_w(0, 1, 1)
+        load_w(1, 0, 0)
+        load_w(1, 1, 0)
+        load_w(1, 0, 1)
+        load_w(1, 1, 1)
+        load_q(1)
+        with nc.allow_non_contiguous_dma(reason="one value of unit a partition"):
+            nc.sync.dma_start(out=unit_t[:], in_=unit.rearrange("(t p) o -> p (t o)", p=P))
+        load_q(2)
+        load_q(3)
+        nc.sync.dma_start(out=w3raw[:], in_=w3.rearrange("(p j) c -> p j c", j=PACK))
+
+        def open_key_window(t):
+            kwin[t] = keep.tile([P, KEY_WINDOW], F32, name="kwin%d" % t, tag="kwin%d" % t, align_bytes=64)
+            nc.gpsimd.memset(kwin[t][:, V:], 0.0)
+
+        open_key_window(0)
+        make_identity(nc, ident[:])
+        for t in range(TILES):
+            nc.gpsimd.memset(vwin[t][:, V:], 0.0)
+
+        gs = keep.tile([P, S], U8, name="gs", align_bytes=64)
+        ds = keep.tile([P, D, V], U8, name="ds", align_bytes=64)
+        gw = {}
+        dw = [keep.tile([P, D, V], U32, name="dw%d" % o, align_bytes=64) for o in range(PASSES)]
+
+        def gather_words(o):
+            gw[o] = keep.tile([P, S], U32, name="gw%d" % o, tag=("gw0", "wgroup000")[o], align_bytes=64)
+            nc.vector.tensor_copy(gw[o][:], xw[o][:].indirect(offs_t[:]))
+
+        def deal_words(o):
+            nc.vector.tensor_copy(
+                out=dw[o][:].rearrange("p d (a i) -> p a d i", i=4),
+                in_=gw[o][:].rearrange("p (a i d) -> p a d i", i=4, d=D),
+            )
+
+        wq, wsc = {}, {}
+
+        def cast_w(m, o, c):
+            g = keep.tile([P, WCOLS, PACK], BF16, name="wgroup%d%d%d" % (m, o, c), tag="wgroup%d%d%d" % (m, o, c), align_bytes=64)
+            nc.scalar.copy(out=g[:], in_=wraw[m, o, c][:].rearrange("p j c -> p c j"))
+            return g
+
+        def quant_w(m, o, c, g):
+            wq[m, o, c] = keep.tile([P, WCOLS], U32, name="wq%d%d%d" % (m, o, c), align_bytes=64)
+            wsc[m, o, c] = keep.tile([P, WCOLS], U8, name="wsc%d%d%d" % (m, o, c), align_bytes=64)
+            nc.vector.quantize_mx(out=wq[m, o, c][:].bitcast(FP8X4), scales=wsc[m, o, c][:], in_=g[:].rearrange("p c j -> p (c j)"))
+
+        def product(m, t):
+            acc = bank((0, 1, 6, 7)[t], [P, V], "acc%d%d" % (m, t))
+            c, cols = t // 2, slice((t % 2) * P, (t % 2 + 1) * P)
+            for o in range(PASSES):
+                for d in range(D):
+                    nc.tensor.matmul_mx(
+                        out=acc[:],
+                        lhsT=wq[m, o, c][:, cols].bitcast(FP8X4),
+                        lhsT_scale=wsc[m, o, c][:, cols],
+                        rhs=dw[o][:, d, :].bitcast(FP8X4),
+                        rhs_scale=ds[4 * o : P, d, :],
+                        start=(o == 0 and d == 0),
+                        stop=(o == PASSES - 1 and d == D - 1),
+                    )
+            return acc
+
+        nc.vector.tensor_copy(gs[:], xs[:].indirect(offs_t[:]))
+        quant_w(0, 0, 0, cast_w(0, 0, 0))
+        nc.vector.tensor_copy(out=ds[:].rearrange("p d (a i) -> p a d i", i=16), in_=gs[:].rearrange("p (a i d) -> p a d i", i=16, d=D))
+        gather_words(0)
+        deal_words(0)
+        gather_words(1)
+        g = cast_w(0, 1, 0)
+        deal_words(1)
+        quant_w(0, 1, 0, g)
+
+        e = [keep.tile([P, LISTS, U], F32, name="e%d" % t, align_bytes=64) for t in range(TILES)]
+        den, args = [], []
+
+        def keys(t):
+            a = keep.tile([P, LISTS, U], F32, name="arg%d" % t, tag=("wgroup011", "arg1", "wgroup110", "wgroup111")[t], align_bytes=64)
+            for l in range(LISTS):
+                nc.vector.tensor_tensor(a[:, l, :], kwin[t][:].indirect(lists[l][:]), q[t][:], MULT)
+            th = keep.tile([P, LISTS, U], F32, name="th%d" % t, tag="bounded", align_bytes=64)
+            for l in range(LISTS):
+                nc.scalar.activation(th[:, l, :], a[:, l, :], ACT.Tanh, scale=1.0 / D)
+            for l in range(LISTS):
+                nc.scalar.activation(e[t][:, l, :], th[:, l, :], ACT.Exp)
+            dsum = bank(2 + t, [P, U // P, P], "den%d" % t)
+            for rb in range(U // P):
+                for l in range(LISTS):
+                    nc.tensor.matmul(dsum[:, rb, :], lhsT=e[t][:, l, rb * P : (rb + 1) * P], rhs=ident[:], is_transpose=True, start=(l == 0), stop=(l == LISTS - 1))
+            den.append(dsum)
+            args.append(a)
+
+        def key_window(t):
+            open_key_window(t)
+            nc.scalar.copy(out=kwin[t][:, :V], in_=key[t][:])
+
+        def val_window(t, acc):
+            nc.scalar.activation(vwin[t][:, :V], acc[:], ACT.Copy, scale=unit_t[:, t : t + 1])
+
+        key = [product(0, 0), product(0, 1)]
+        nc.vector.tensor_copy(out=kwin[0][:, :V], in_=key[0][:])
+        for o in range(PASSES):
+            quant_w(0, o, 1, cast_w(0, o, 1))
+        key.extend([product(0, 2), product(0, 3)])
+        for n, (o, c) in enumerate(((0, 0), (1, 0), (0, 1), (1, 1))):
+            quant_w(1, o, c, cast_w(1, o, c))
+            if n + 1 < TILES:
+                key_window(n + 1)
+        val = [product(1, t) for t in range(TILES)]
+        keys(0)
+        keys(1)
+        val_window(0, val[0])
+        val_window(1, val[1])
+        keys(2)
+        val_window(2, val[2])
+        val_window(3, val[3])
+        keys(3)
+
+        logden = keep.tile([P, 2, TILES, HALF], F32, name="logden", tag="bounded", align_bytes=64)
+        for t in range(TILES):
+            nc.scalar.activation(logden[:, :, t, :], den[t][:].rearrange("p (h b) f -> p h (b f)", h=2), ACT.Ln, scale=float(D))
+        recip = [keep.tile([P, 2, TILES, P], F32, name="recip%d" % h, tag="recip%d" % h, align_bytes=64) for h in range(2)]
+        for h in range(2):
+            nc.scalar.activation(recip[h][:].rearrange("r u t (g e) -> r u (t g) e", e=2), logden[:, h, :, :].rearrange("r t (g u e) -> r u (t g) e", u=2, e=2), ACT.Exp, scale=-1.0)
+
+        w3g = keep.tile([P, N, PACK], BF16, name="w3g", tag="w3g", align_bytes=64)
+        nc.scalar.copy(out=w3g[:], in_=w3raw[:].rearrange("p j c -> p c j"))
+        w3q = keep.tile([P, N], U32, name="w3q", align_bytes=64)
+        w3s = keep.tile([P, N], U8, name="w3s", align_bytes=64)
+        nc.vector.quantize_mx(out=w3q[:].bitcast(FP8X4), scales=w3s[:], in_=w3g[:].rearrange("p c j -> p (c j)"))
+        early = keep.tile([P, TILES, LISTS, HALF], F32, name="terms_early", tag="kwin3", align_bytes=64)
+        middle = keep.tile([P, 2, LISTS, HALF], F32, name="terms_middle", tag="q3", align_bytes=64)
+        late = keep.tile([P, 2, LISTS, HALF], F32, name="terms_late", tag="recip0", align_bytes=64)
+        for h in range(2):
+            hid_t = keep.tile([P, 2, 2, TILES, 32, 2], BF16, name="hid_t%d" % h, align_bytes=64)
+            for t in range(TILES):
+                terms = early[:, t] if h == 0 else (middle[:, t] if t < 2 else late[:, t - 2])
+                for l in range(LISTS):
+                    nc.vector.tensor_tensor(terms[:, l, :], vwin[t][:].indirect(lists[l][:, h * 16 : (h + 1) * 16]), e[t][:, l, h * HALF : (h + 1) * HALF], MULT)
+                nsum = bank(2 + t, [P, 2, P], "num%d%d" % (h, t))
+                for rb in range(2):
+                    for l in range(LISTS):
+                        nc.tensor.matmul(nsum[:, rb, :], lhsT=terms[:, l, rb * P : (rb + 1) * P], rhs=ident[:], is_transpose=True, start=(l == 0), stop=(l == LISTS - 1))
+                nc.vector.tensor_tensor(
+                    hid_t[:, :, :, t, :, :],
+                    nsum[:].rearrange("r b (g u e) -> r u b g e", u=2, e=2),
+                    recip[h][:, :, t, :].rearrange("r u (b g e) -> r u b g e", b=2, e=2),
+                    MULT,
+                )
+            words = hid_t[:].rearrange("r u b t g e -> r u b (t g e)").bitcast(F32)
+            back = bank(6 + h, [P, 2, 2, P], "back%d" % h)
+            for u in range(2):
+                for rb in range(2):
+                    nc.tensor.transpose(back[:, u, rb, :], words[:, u, rb, :], ident[:])
+            hid = keep.tile([P, HALF * PACK], BF16, name="hid%d" % h, align_bytes=64)
+            nc.scalar.copy(out=hid[:].bitcast(F32).rearrange("p (r u) -> p r u", u=2), in_=back[:].rearrange("p u b r -> p (b r) u"))
+            hq = keep.tile([P, HALF], U32, name="hq%d" % h, align_bytes=64)
+            hs = keep.tile([P, HALF], U8, name="hs%d" % h, align_bytes=64)
+            nc.vector.quantize_mx(out=hq[:].bitcast(FP8X4), scales=hs[:], in_=hid[:])
+            res = bank(h, [P, HALF], "res%d" % h)
+            nc.tensor.matmul_mx(out=res[:], lhsT=w3q[:].bitcast(FP8X4), lhsT_scale=w3s[:], rhs=hq[:].bitcast(FP8X4), rhs_scale=hs[:], start=True, stop=True)
+            staged = keep.tile([P, HALF], F32, name="staged%d" % h, align_bytes=64)
+            nc.scalar.copy(out=staged[:], in_=res[:])
+            nc.sync.dma_start(out=out[:, h * HALF : (h + 1) * HALF], in_=staged[:])

@@ -23,8 +23,7 @@ TILES = H // P
 LISTS = 3
 WCOLS = 256
 HALF = U // 2
-KEY_WINDOW = U + 16
-VAL_WINDOW = HALF + 16
+WINDOW = U + 16
 
 
 def tile_picked_ymoba_avg_p_kernel(tc, x_words, x_scales, w1, w2, qry, unit, w3, offs, b1, b2, b3, out):
@@ -38,26 +37,29 @@ def tile_picked_ymoba_avg_p_kernel(tc, x_words, x_scales, w1, w2, qry, unit, w3,
 
         offs_t = keep.tile([P, S // 16], U16, name="offs_t")
         lists = [keep.tile([P, U // 16], U16, name="list%d" % l) for l in range(LISTS)]
-        xw = [keep.tile([P, T], U32, name="xw%d" % o, align_bytes=64) for o in range(PASSES)]
+        xw = [keep.tile([P, T], U32, name="xw%d" % o, tag="xw%d" % o, align_bytes=64) for o in range(PASSES)]
         xs = keep.tile([P, T], U8, name="xs", align_bytes=64)
         ident = keep.tile([P, P], F32, name="ident")
         kwin = {}
-        vwin = [keep.tile([P, VAL_WINDOW], F32, name="vwin%d" % t, align_bytes=64) for t in range(TILES)]
+        vwin = [keep.tile([P, WINDOW], F32, name="vwin%d" % t, align_bytes=64) for t in range(TILES)]
         q = [keep.tile([P, U], F32, name="q%d" % t, tag="q%d" % t, align_bytes=64) for t in range(TILES)]
         unit_t = keep.tile([P, TILES], F32, name="unit_t")
+        w1raw = [keep.tile([P, PACK, H], F32, name="w1raw%d" % o, align_bytes=64) for o in range(PASSES)]
         wraw = {}
-        for m in range(2):
-            for o in range(PASSES):
-                for c in range(2):
-                    wraw[m, o, c] = keep.tile([P, PACK, WCOLS], F32, name="wraw%d%d%d" % (m, o, c), tag=({(1, 0, 0): "kwin1", (1, 1, 0): "kwin2", (1, 0, 1): "kwin3", (1, 1, 1): "bounded"}.get((m, o, c), "wraw%d%d%d" % (m, o, c))), align_bytes=64)
+        for o in range(PASSES):
+            for c in range(2):
+                wraw[0, o, c] = w1raw[o][:, :, c * WCOLS : (c + 1) * WCOLS]
+                wraw[1, o, c] = keep.tile([P, PACK, WCOLS], F32, name="w2raw%d%d" % (o, c), tag=("kwin1", "kwin3", "kwin2", "bounded")[2 * o + c], align_bytes=64)[:]
         w3raw = keep.tile([P, PACK, N], F32, name="w3raw", align_bytes=64)
 
         nc.gpsimd.memset(xs[:].bitcast(I32), 0)
 
-        def load_w(m, o, c):
-            w = (w1, w2)[m]
-            rows = w[o * P * PACK : (o + 1) * P * PACK, c * WCOLS : (c + 1) * WCOLS]
-            nc.sync.dma_start(out=wraw[m, o, c][:], in_=rows.rearrange("(p j) c -> p j c", j=PACK))
+        def load_w1(o):
+            nc.sync.dma_start(out=w1raw[o][:], in_=w1[o * P * PACK : (o + 1) * P * PACK, :].rearrange("(p j) c -> p j c", j=PACK))
+
+        def load_w2(o, c):
+            rows = w2[o * P * PACK : (o + 1) * P * PACK, c * WCOLS : (c + 1) * WCOLS]
+            nc.sync.dma_start(out=wraw[1, o, c], in_=rows.rearrange("(p j) c -> p j c", j=PACK))
 
         def load_x(o):
             nc.sync.dma_start(out=xw[o][:].bitcast(I32), in_=x_words[o].rearrange("p n t -> p (n t)").bitcast(I32))
@@ -66,22 +68,19 @@ def tile_picked_ymoba_avg_p_kernel(tc, x_words, x_scales, w1, w2, qry, unit, w3,
             nc.sync.dma_start(out=q[t][:], in_=qry[t * P : (t + 1) * P, :])
 
         nc.sync.dma_start(offs_t[:], offs)
-        load_w(0, 0, 0)
+        load_x(0)
         for quad in range(4):
             nc.sync.dma_start(out=xs[32 * quad : 32 * quad + 8, :].bitcast(I32), in_=x_scales[:, 4 * quad : 4 * quad + 4, :].bitcast(I32))
-        load_x(0)
+        load_w1(0)
         load_x(1)
-        load_w(0, 1, 0)
+        load_w1(1)
         nc.sync.dma_start(lists[0][:], b1)
         load_q(0)
         nc.sync.dma_start(lists[1][:], b2)
         nc.sync.dma_start(lists[2][:], b3)
-        load_w(0, 0, 1)
-        load_w(0, 1, 1)
-        load_w(1, 0, 0)
-        load_w(1, 1, 0)
-        load_w(1, 0, 1)
-        load_w(1, 1, 1)
+        for c in range(2):
+            for o in range(PASSES):
+                load_w2(o, c)
         load_q(1)
         with nc.allow_non_contiguous_dma(reason="one value of unit a partition"):
             nc.sync.dma_start(out=unit_t[:], in_=unit.rearrange("(t p) o -> p (t o)", p=P))
@@ -90,7 +89,7 @@ def tile_picked_ymoba_avg_p_kernel(tc, x_words, x_scales, w1, w2, qry, unit, w3,
         nc.sync.dma_start(out=w3raw[:], in_=w3.rearrange("(p j) c -> p j c", j=PACK))
 
         def open_key_window(t):
-            kwin[t] = keep.tile([P, KEY_WINDOW], F32, name="kwin%d" % t, tag="kwin%d" % t, align_bytes=64)
+            kwin[t] = keep.tile([P, WINDOW], F32, name="kwin%d" % t, tag="kwin%d" % t, align_bytes=64)
             nc.gpsimd.memset(kwin[t][:, V:], 0.0)
 
         open_key_window(0)
@@ -117,11 +116,11 @@ def tile_picked_ymoba_avg_p_kernel(tc, x_words, x_scales, w1, w2, qry, unit, w3,
 
         def cast_w(m, o, c):
             g = keep.tile([P, WCOLS, PACK], BF16, name="wgroup%d%d%d" % (m, o, c), tag="wgroup%d%d%d" % (m, o, c), align_bytes=64)
-            nc.scalar.copy(out=g[:], in_=wraw[m, o, c][:].rearrange("p j c -> p c j"))
+            nc.scalar.copy(out=g[:].rearrange("p (a i) j -> p a j i", i=4), in_=wraw[m, o, c].rearrange("p j (a i) -> p a j i", i=4))
             return g
 
         def quant_w(m, o, c, g):
-            wq[m, o, c] = keep.tile([P, WCOLS], U32, name="wq%d%d%d" % (m, o, c), align_bytes=64)
+            wq[m, o, c] = keep.tile([P, WCOLS], U32, name="wq%d%d%d" % (m, o, c), tag=("xw1" if (m, o, c) == (0, 0, 1) else "wq%d%d%d" % (m, o, c)), align_bytes=64)
             wsc[m, o, c] = keep.tile([P, WCOLS], U8, name="wsc%d%d%d" % (m, o, c), align_bytes=64)
             nc.vector.quantize_mx(out=wq[m, o, c][:].bitcast(FP8X4), scales=wsc[m, o, c][:], in_=g[:].rearrange("p c j -> p (c j)"))
 
@@ -141,15 +140,17 @@ def tile_picked_ymoba_avg_p_kernel(tc, x_words, x_scales, w1, w2, qry, unit, w3,
                     )
             return acc
 
-        nc.vector.tensor_copy(gs[:], xs[:].indirect(offs_t[:]))
-        quant_w(0, 0, 0, cast_w(0, 0, 0))
-        nc.vector.tensor_copy(out=ds[:].rearrange("p d (a i) -> p a d i", i=16), in_=gs[:].rearrange("p (a i d) -> p a d i", i=16, d=D))
         gather_words(0)
+        nc.vector.tensor_copy(gs[:], xs[:].indirect(offs_t[:]))
         deal_words(0)
+        nc.vector.tensor_copy(out=ds[:].rearrange("p d (a i) -> p a d i", i=16), in_=gs[:].rearrange("p (a i d) -> p a d i", i=16, d=D))
+        quant_w(0, 0, 0, cast_w(0, 0, 0))
+        g01 = cast_w(0, 0, 1)
         gather_words(1)
-        g = cast_w(0, 1, 0)
+        quant_w(0, 1, 0, cast_w(0, 1, 0))
         deal_words(1)
-        quant_w(0, 1, 0, g)
+        quant_w(0, 0, 1, g01)
+        quant_w(0, 1, 1, cast_w(0, 1, 1))
 
         e = [keep.tile([P, LISTS, U], F32, name="e%d" % t, align_bytes=64) for t in range(TILES)]
         den, args = [], []
@@ -158,7 +159,6 @@ def tile_picked_ymoba_avg_p_kernel(tc, x_words, x_scales, w1, w2, qry, unit, w3,
             a = keep.tile([P, LISTS, U], F32, name="arg%d" % t, tag=("wgroup011", "arg1", "wgroup110", "wgroup111")[t], align_bytes=64)
             for l in range(LISTS):
                 nc.vector.tensor_tensor(a[:, l, :], kwin[t][:].indirect(lists[l][:]), q[t][:], MULT)
-            th = keep.tile([P, LISTS, U], F32, name="th%d" % t, tag="bounded", align_bytes=64)
             for l in range(LISTS):
                 nc.scalar.activation(th[:, l, :], a[:, l, :], ACT.Tanh, scale=1.0 / D)
             for l in range(LISTS):
@@ -179,14 +179,13 @@ def tile_picked_ymoba_avg_p_kernel(tc, x_words, x_scales, w1, w2, qry, unit, w3,
 
         key = [product(0, 0), product(0, 1)]
         nc.vector.tensor_copy(out=kwin[0][:, :V], in_=key[0][:])
-        for o in range(PASSES):
-            quant_w(0, o, 1, cast_w(0, o, 1))
         key.extend([product(0, 2), product(0, 3)])
         for n, (o, c) in enumerate(((0, 0), (1, 0), (0, 1), (1, 1))):
             quant_w(1, o, c, cast_w(1, o, c))
             if n + 1 < TILES:
                 key_window(n + 1)
         val = [product(1, t) for t in range(TILES)]
+        th = keep.tile([P, LISTS, U], F32, name="th", tag="bounded", align_bytes=64)
         keys(0)
         keys(1)
         val_window(0, val[0])
@@ -204,41 +203,78 @@ def tile_picked_ymoba_avg_p_kernel(tc, x_words, x_scales, w1, w2, qry, unit, w3,
             nc.scalar.activation(recip[h][:].rearrange("r u t (g e) -> r u (t g) e", e=2), logden[:, h, :, :].rearrange("r t (g u e) -> r u (t g) e", u=2, e=2), ACT.Exp, scale=-1.0)
 
         w3g = keep.tile([P, N, PACK], BF16, name="w3g", tag="w3g", align_bytes=64)
-        nc.scalar.copy(out=w3g[:], in_=w3raw[:].rearrange("p j c -> p c j"))
+        nc.scalar.copy(out=w3g[:].rearrange("p (a i) j -> p a j i", i=4), in_=w3raw[:].rearrange("p j (a i) -> p a j i", i=4))
         w3q = keep.tile([P, N], U32, name="w3q", align_bytes=64)
         w3s = keep.tile([P, N], U8, name="w3s", align_bytes=64)
         nc.vector.quantize_mx(out=w3q[:].bitcast(FP8X4), scales=w3s[:], in_=w3g[:].rearrange("p c j -> p (c j)"))
-        early = keep.tile([P, TILES, LISTS, HALF], F32, name="terms_early", tag="kwin3", align_bytes=64)
-        middle = keep.tile([P, 2, LISTS, HALF], F32, name="terms_middle", tag="q3", align_bytes=64)
-        late = keep.tile([P, 2, LISTS, HALF], F32, name="terms_late", tag="recip0", align_bytes=64)
-        for h in range(2):
-            hid_t = keep.tile([P, 2, 2, TILES, 32, 2], BF16, name="hid_t%d" % h, align_bytes=64)
-            for t in range(TILES):
-                terms = early[:, t] if h == 0 else (middle[:, t] if t < 2 else late[:, t - 2])
-                for l in range(LISTS):
-                    nc.vector.tensor_tensor(terms[:, l, :], vwin[t][:].indirect(lists[l][:, h * 16 : (h + 1) * 16]), e[t][:, l, h * HALF : (h + 1) * HALF], MULT)
-                nsum = bank(2 + t, [P, 2, P], "num%d%d" % (h, t))
-                for rb in range(2):
-                    for l in range(LISTS):
-                        nc.tensor.matmul(nsum[:, rb, :], lhsT=terms[:, l, rb * P : (rb + 1) * P], rhs=ident[:], is_transpose=True, start=(l == 0), stop=(l == LISTS - 1))
-                nc.vector.tensor_tensor(
-                    hid_t[:, :, :, t, :, :],
-                    nsum[:].rearrange("r b (g u e) -> r u b g e", u=2, e=2),
-                    recip[h][:, :, t, :].rearrange("r u (b g e) -> r u b g e", b=2, e=2),
-                    MULT,
-                )
-            words = hid_t[:].rearrange("r u b t g e -> r u b (t g e)").bitcast(F32)
-            back = bank(6 + h, [P, 2, 2, P], "back%d" % h)
-            for u in range(2):
-                for rb in range(2):
-                    nc.tensor.transpose(back[:, u, rb, :], words[:, u, rb, :], ident[:])
-            hid = keep.tile([P, HALF * PACK], BF16, name="hid%d" % h, align_bytes=64)
+        last = TILES - 1
+        early = keep.tile([P, last, LISTS, U], F32, name="terms_early", tag="kwin3", align_bytes=64)
+        middle = keep.tile([P, LISTS, HALF], F32, name="terms_middle", tag="q3", align_bytes=64)
+        hid_t = [keep.tile([P, 2, 2, TILES, 32, 2], BF16, name="hid_t%d" % h, align_bytes=64) for h in range(2)]
+
+        def weigh(terms, t, first, count):
+            for l in range(LISTS):
+                offsets = lists[l][:, first // 16 : (first + count) // 16]
+                nc.vector.tensor_tensor(terms[:, l, :], vwin[t][:].indirect(offsets), e[t][:, l, first : first + count], MULT)
+
+        def add_up(dst, terms, l, rb):
+            nc.tensor.matmul(dst, lhsT=terms[:, l, rb * P : (rb + 1) * P], rhs=ident[:], is_transpose=True, start=(l == 0), stop=(l == LISTS - 1))
+
+        def normalise(nsum, h, t, blocks):
+            nc.vector.tensor_tensor(
+                hid_t[h][:, :, blocks, t, :, :],
+                nsum.rearrange("r b (g u e) -> r u b g e", u=2, e=2),
+                recip[h][:, :, t, :].rearrange("r u (b g e) -> r u b g e", b=2, e=2)[:, :, blocks],
+                MULT,
+            )
+
+        def project(h, blocks, back_bank, res_bank):
+            count = blocks.stop - blocks.start
+            width = count * P
+            first = h * HALF + blocks.start * P
+            words = hid_t[h][:].rearrange("r u b t g e -> r u b (t g e)").bitcast(F32)
+            back = bank(back_bank, [P, 2, count, P], "back%d" % first)
+            for rb in range(count):
+                for u in range(2):
+                    nc.tensor.transpose(back[:, u, rb, :], words[:, u, blocks.start + rb, :], ident[:])
+            hid = keep.tile([P, width * PACK], BF16, name="hid%d" % first, align_bytes=64)
             nc.scalar.copy(out=hid[:].bitcast(F32).rearrange("p (r u) -> p r u", u=2), in_=back[:].rearrange("p u b r -> p (b r) u"))
-            hq = keep.tile([P, HALF], U32, name="hq%d" % h, align_bytes=64)
-            hs = keep.tile([P, HALF], U8, name="hs%d" % h, align_bytes=64)
+            hq = keep.tile([P, width], U32, name="hq%d" % first, align_bytes=64)
+            hs = keep.tile([P, width], U8, name="hs%d" % first, align_bytes=64)
             nc.vector.quantize_mx(out=hq[:].bitcast(FP8X4), scales=hs[:], in_=hid[:])
-            res = bank(h, [P, HALF], "res%d" % h)
+            res = bank(res_bank, [P, width], "res%d" % first)
             nc.tensor.matmul_mx(out=res[:], lhsT=w3q[:].bitcast(FP8X4), lhsT_scale=w3s[:], rhs=hq[:].bitcast(FP8X4), rhs_scale=hs[:], start=True, stop=True)
-            staged = keep.tile([P, HALF], F32, name="staged%d" % h, align_bytes=64)
+            staged = keep.tile([P, width], F32, name="staged%d" % first, align_bytes=64)
             nc.scalar.copy(out=staged[:], in_=res[:])
-            nc.sync.dma_start(out=out[:, h * HALF : (h + 1) * HALF], in_=staged[:])
+            nc.sync.dma_start(out=out[:, first : first + width], in_=staged[:])
+
+        num = []
+        for t in range(last):
+            weigh(early[:, t], t, 0, U)
+            nsum = bank((0, 2, 3)[t], [P, U // P, P], "num%d" % t)
+            for rb in range(U // P):
+                for l in range(LISTS):
+                    add_up(nsum[:, rb, :], early[:, t], l, rb)
+            num.append(nsum)
+        weigh(middle, last, 0, HALF)
+        nsum = bank(4, [P, 2, P], "num_middle")
+        for rb in range(2):
+            for l in range(LISTS):
+                add_up(nsum[:, rb, :], middle, l, rb)
+        both = slice(0, 2)
+        for t in range(last):
+            normalise(num[t][:, 0:2, :], 0, t, both)
+        normalise(nsum[:], 0, last, both)
+        project(0, both, 6, 4)
+        for t in range(last):
+            normalise(num[t][:, 2:4, :], 1, t, both)
+        late = keep.tile([P, LISTS, HALF], F32, name="terms_late", tag="recip0", align_bytes=64)
+        weigh(late, last, HALF, HALF)
+        ends = [bank((5, 1)[rb], [P, 1, P], "num_late%d" % rb) for rb in range(2)]
+        for l in range(LISTS):
+            for rb in range(2):
+                add_up(ends[rb][:, 0, :], late, l, rb)
+        for rb in range(2):
+            normalise(ends[rb][:], 1, last, slice(rb, rb + 1))
+        for rb in range(2):
+            project(1, slice(rb, rb + 1), (7, 6)[rb], (0, 2)[rb])

@@ -37,29 +37,25 @@ def tile_picked_ymoba_avg_p_kernel(tc, x_words, x_scales, w1, w2, qry, unit, w3,
 
         offs_t = keep.tile([P, S // 16], U16, name="offs_t")
         lists = [keep.tile([P, U // 16], U16, name="list%d" % l) for l in range(LISTS)]
-        xw = [keep.tile([P, T], U32, name="xw%d" % o, tag="xw%d" % o, align_bytes=64) for o in range(PASSES)]
+        xw = [keep.tile([P, T], U32, name="xw%d" % o, align_bytes=64) for o in range(PASSES)]
         xs = keep.tile([P, T], U8, name="xs", align_bytes=64)
         ident = keep.tile([P, P], F32, name="ident")
         kwin = {}
         vwin = [keep.tile([P, WINDOW], F32, name="vwin%d" % t, align_bytes=64) for t in range(TILES)]
         q = [keep.tile([P, U], F32, name="q%d" % t, tag="q%d" % t, align_bytes=64) for t in range(TILES)]
         unit_t = keep.tile([P, TILES], F32, name="unit_t")
-        w1raw = [keep.tile([P, PACK, H], F32, name="w1raw%d" % o, align_bytes=64) for o in range(PASSES)]
         wraw = {}
         for o in range(PASSES):
             for c in range(2):
-                wraw[0, o, c] = w1raw[o][:, :, c * WCOLS : (c + 1) * WCOLS]
+                wraw[0, o, c] = keep.tile([P, PACK, WCOLS], F32, name="w1raw%d%d" % (o, c), align_bytes=64)[:]
                 wraw[1, o, c] = keep.tile([P, PACK, WCOLS], F32, name="w2raw%d%d" % (o, c), tag=("kwin1", "kwin3", "kwin2", "bounded")[2 * o + c], align_bytes=64)[:]
         w3raw = keep.tile([P, PACK, N], F32, name="w3raw", align_bytes=64)
 
         nc.gpsimd.memset(xs[:].bitcast(I32), 0)
 
-        def load_w1(o):
-            nc.sync.dma_start(out=w1raw[o][:], in_=w1[o * P * PACK : (o + 1) * P * PACK, :].rearrange("(p j) c -> p j c", j=PACK))
-
-        def load_w2(o, c):
-            rows = w2[o * P * PACK : (o + 1) * P * PACK, c * WCOLS : (c + 1) * WCOLS]
-            nc.sync.dma_start(out=wraw[1, o, c], in_=rows.rearrange("(p j) c -> p j c", j=PACK))
+        def load_w(m, o, c):
+            rows = (w1, w2)[m][o * P * PACK : (o + 1) * P * PACK, c * WCOLS : (c + 1) * WCOLS]
+            nc.sync.dma_start(out=wraw[m, o, c], in_=rows.rearrange("(p j) c -> p j c", j=PACK))
 
         def load_x(o):
             nc.sync.dma_start(out=xw[o][:].bitcast(I32), in_=x_words[o].rearrange("p n t -> p (n t)").bitcast(I32))
@@ -68,19 +64,20 @@ def tile_picked_ymoba_avg_p_kernel(tc, x_words, x_scales, w1, w2, qry, unit, w3,
             nc.sync.dma_start(out=q[t][:], in_=qry[t * P : (t + 1) * P, :])
 
         nc.sync.dma_start(offs_t[:], offs)
-        load_x(0)
+        load_q(0)
         for quad in range(4):
             nc.sync.dma_start(out=xs[32 * quad : 32 * quad + 8, :].bitcast(I32), in_=x_scales[:, 4 * quad : 4 * quad + 4, :].bitcast(I32))
-        load_w1(0)
+        load_x(0)
+        load_w(0, 0, 0)
         load_x(1)
-        load_w1(1)
-        nc.sync.dma_start(lists[0][:], b1)
-        load_q(0)
-        nc.sync.dma_start(lists[1][:], b2)
-        nc.sync.dma_start(lists[2][:], b3)
+        load_w(0, 1, 0)
+        for offsets, source in zip(lists, (b1, b2, b3)):
+            nc.sync.dma_start(offsets[:], source)
+        for o in range(PASSES):
+            load_w(0, o, 1)
         for c in range(2):
             for o in range(PASSES):
-                load_w2(o, c)
+                load_w(1, o, c)
         load_q(1)
         with nc.allow_non_contiguous_dma(reason="one value of unit a partition"):
             nc.sync.dma_start(out=unit_t[:], in_=unit.rearrange("(t p) o -> p (t o)", p=P))
@@ -120,7 +117,7 @@ def tile_picked_ymoba_avg_p_kernel(tc, x_words, x_scales, w1, w2, qry, unit, w3,
             return g
 
         def quant_w(m, o, c, g):
-            wq[m, o, c] = keep.tile([P, WCOLS], U32, name="wq%d%d%d" % (m, o, c), tag=("xw1" if (m, o, c) == (0, 0, 1) else "wq%d%d%d" % (m, o, c)), align_bytes=64)
+            wq[m, o, c] = keep.tile([P, WCOLS], U32, name="wq%d%d%d" % (m, o, c), align_bytes=64)
             wsc[m, o, c] = keep.tile([P, WCOLS], U8, name="wsc%d%d%d" % (m, o, c), align_bytes=64)
             nc.vector.quantize_mx(out=wq[m, o, c][:].bitcast(FP8X4), scales=wsc[m, o, c][:], in_=g[:].rearrange("p c j -> p (c j)"))
 
@@ -140,17 +137,16 @@ def tile_picked_ymoba_avg_p_kernel(tc, x_words, x_scales, w1, w2, qry, unit, w3,
                     )
             return acc
 
-        gather_words(0)
         nc.vector.tensor_copy(gs[:], xs[:].indirect(offs_t[:]))
-        deal_words(0)
         nc.vector.tensor_copy(out=ds[:].rearrange("p d (a i) -> p a d i", i=16), in_=gs[:].rearrange("p (a i d) -> p a d i", i=16, d=D))
+        gather_words(0)
         quant_w(0, 0, 0, cast_w(0, 0, 0))
-        g01 = cast_w(0, 0, 1)
+        deal_words(0)
         gather_words(1)
         quant_w(0, 1, 0, cast_w(0, 1, 0))
         deal_words(1)
-        quant_w(0, 0, 1, g01)
-        quant_w(0, 1, 1, cast_w(0, 1, 1))
+        for o in range(PASSES):
+            quant_w(0, o, 1, cast_w(0, o, 1))
 
         e = [keep.tile([P, LISTS, U], F32, name="e%d" % t, align_bytes=64) for t in range(TILES)]
         den, args = [], []
@@ -204,31 +200,27 @@ def tile_picked_ymoba_avg_p_kernel(tc, x_words, x_scales, w1, w2, qry, unit, w3,
 
         w3g = keep.tile([P, N, PACK], BF16, name="w3g", tag="w3g", align_bytes=64)
         nc.scalar.copy(out=w3g[:].rearrange("p (a i) j -> p a j i", i=4), in_=w3raw[:].rearrange("p j (a i) -> p a j i", i=4))
-        w3q = keep.tile([P, N], U32, name="w3q", align_bytes=64)
-        w3s = keep.tile([P, N], U8, name="w3s", align_bytes=64)
-        nc.vector.quantize_mx(out=w3q[:].bitcast(FP8X4), scales=w3s[:], in_=w3g[:].rearrange("p c j -> p (c j)"))
         last = TILES - 1
-        early = keep.tile([P, last, LISTS, U], F32, name="terms_early", tag="kwin3", align_bytes=64)
-        middle = keep.tile([P, LISTS, HALF], F32, name="terms_middle", tag="q3", align_bytes=64)
+        terms = keep.tile([P, TILES, LISTS, U], F32, name="terms", tag="kwin3", align_bytes=64)
         hid_t = [keep.tile([P, 2, 2, TILES, 32, 2], BF16, name="hid_t%d" % h, align_bytes=64) for h in range(2)]
 
-        def weigh(terms, t, first, count):
-            for l in range(LISTS):
-                offsets = lists[l][:, first // 16 : (first + count) // 16]
-                nc.vector.tensor_tensor(terms[:, l, :], vwin[t][:].indirect(offsets), e[t][:, l, first : first + count], MULT)
+        def add_up(b, t, first, count):
+            nsum = bank(b, [P, count, P], "num%d%d" % (t, first))
+            for rb in range(count):
+                for l in range(LISTS):
+                    cols = slice((first + rb) * P, (first + rb + 1) * P)
+                    nc.tensor.matmul(nsum[:, rb, :], lhsT=terms[:, t, l, cols], rhs=ident[:], is_transpose=True, start=(l == 0), stop=(l == LISTS - 1))
+            return nsum
 
-        def add_up(dst, terms, l, rb):
-            nc.tensor.matmul(dst, lhsT=terms[:, l, rb * P : (rb + 1) * P], rhs=ident[:], is_transpose=True, start=(l == 0), stop=(l == LISTS - 1))
-
-        def normalise(nsum, h, t, blocks):
+        def normalise(nsum, h, t):
             nc.vector.tensor_tensor(
-                hid_t[h][:, :, blocks, t, :, :],
+                hid_t[h][:, :, :, t, :, :],
                 nsum.rearrange("r b (g u e) -> r u b g e", u=2, e=2),
-                recip[h][:, :, t, :].rearrange("r u (b g e) -> r u b g e", b=2, e=2)[:, :, blocks],
+                recip[h][:, :, t, :].rearrange("r u (b g e) -> r u b g e", b=2, e=2),
                 MULT,
             )
 
-        def project(h, blocks, back_bank, res_bank):
+        def project(h, blocks, back_bank, res_bank, queue):
             count = blocks.stop - blocks.start
             width = count * P
             first = h * HALF + blocks.start * P
@@ -246,35 +238,23 @@ def tile_picked_ymoba_avg_p_kernel(tc, x_words, x_scales, w1, w2, qry, unit, w3,
             nc.tensor.matmul_mx(out=res[:], lhsT=w3q[:].bitcast(FP8X4), lhsT_scale=w3s[:], rhs=hq[:].bitcast(FP8X4), rhs_scale=hs[:], start=True, stop=True)
             staged = keep.tile([P, width], F32, name="staged%d" % first, align_bytes=64)
             nc.scalar.copy(out=staged[:], in_=res[:])
-            nc.sync.dma_start(out=out[:, first : first + width], in_=staged[:])
+            queue.dma_start(out=out[:, first : first + width], in_=staged[:])
 
-        num = []
-        for t in range(last):
-            weigh(early[:, t], t, 0, U)
-            nsum = bank((0, 2, 3)[t], [P, U // P, P], "num%d" % t)
-            for rb in range(U // P):
-                for l in range(LISTS):
-                    add_up(nsum[:, rb, :], early[:, t], l, rb)
-            num.append(nsum)
-        weigh(middle, last, 0, HALF)
-        nsum = bank(4, [P, 2, P], "num_middle")
-        for rb in range(2):
+        num = {}
+        for t in range(TILES):
             for l in range(LISTS):
-                add_up(nsum[:, rb, :], middle, l, rb)
-        both = slice(0, 2)
-        for t in range(last):
-            normalise(num[t][:, 0:2, :], 0, t, both)
-        normalise(nsum[:], 0, last, both)
-        project(0, both, 6, 4)
-        for t in range(last):
-            normalise(num[t][:, 2:4, :], 1, t, both)
-        late = keep.tile([P, LISTS, HALF], F32, name="terms_late", tag="recip0", align_bytes=64)
-        weigh(late, last, HALF, HALF)
-        ends = [bank((5, 1)[rb], [P, 1, P], "num_late%d" % rb) for rb in range(2)]
-        for l in range(LISTS):
-            for rb in range(2):
-                add_up(ends[rb][:, 0, :], late, l, rb)
+                nc.vector.tensor_tensor(terms[:, t, l, :], vwin[t][:].indirect(lists[l][:]), e[t][:, l, :], MULT)
+            if t < last:
+                nsum = add_up((0, 2, 3)[t], t, 0, 4)
+                num[0, t], num[1, t] = nsum[:, 0:2, :], nsum[:, 2:4, :]
+            else:
+                num[0, t], num[1, t] = add_up(4, t, 0, 2)[:], add_up(5, t, 2, 2)[:]
+        for h in range(2):
+            for t in range(TILES):
+                normalise(num[h, t], h, t)
+        w3q = keep.tile([P, N], U32, name="w3q", align_bytes=64)
+        w3s = keep.tile([P, N], U8, name="w3s", align_bytes=64)
+        nc.vector.quantize_mx(out=w3q[:].bitcast(FP8X4), scales=w3s[:], in_=w3g[:].rearrange("p c j -> p (c j)"))
+        project(0, slice(0, 2), 6, 1, nc.sync)
         for rb in range(2):
-            normalise(ends[rb][:], 1, last, slice(rb, rb + 1))
-        for rb in range(2):
-            project(1, slice(rb, rb + 1), (7, 6)[rb], (0, 2)[rb])
+            project(1, slice(rb, rb + 1), (7, 4)[rb], (0, 2)[rb], (nc.sync, nc.scalar)[rb])

from contextlib import ExitStack

import concourse.mybir as mybir
from concourse.masks import make_identity

K, T, S, D, N, H, V, U = 1024, 2048, 1024, 4, 128, 512, 256, 512
FLOPS = 2 * (2 * K * H * S + H * N * U)

F32 = mybir.dt.float32
BF16 = mybir.dt.bfloat16
I32 = mybir.dt.int32
U32 = mybir.dt.uint32
U16 = mybir.dt.uint16
U8 = mybir.dt.uint8
FP8X4 = mybir.dt.float8_e4m3fn_x4
ACT = mybir.ActivationFunctionType
MULT = mybir.AluOpType.mult

P = 128
PACK = 4
PASSES = K // (P * PACK)
TILES = H // P
LISTS = 3
WCOLS = 256
HALF = U // 2
WINDOW = U + 16


def tile_picked_ymoba_avg_p_kernel(tc, x_words, x_scales, w1, w2, qry, unit, w3, offs, b1, b2, b3, out):
    nc = tc.nc
    with ExitStack() as ctx:
        keep = ctx.enter_context(tc.tile_pool(name="keep", bufs=1))
        psum = ctx.enter_context(tc.psum_pool(name="psum", bufs=1))

        def bank(b, shape, name):
            return psum.tile(shape, F32, name=name, tag="bank%d" % b)

        offs_t = keep.tile([P, S // 16], U16, name="offs_t")
        lists = [keep.tile([P, U // 16], U16, name="list%d" % l) for l in range(LISTS)]
        xw = [keep.tile([P, T], U32, name="xw%d" % o, align_bytes=64) for o in range(PASSES)]
        xs = keep.tile([P, T], U8, name="xs", align_bytes=64)
        ident = keep.tile([P, P], F32, name="ident")
        kwin = {}
        vwin = [keep.tile([P, WINDOW], F32, name="vwin%d" % t, align_bytes=64) for t in range(TILES)]
        q = [keep.tile([P, U], F32, name="q%d" % t, tag="q%d" % t, align_bytes=64) for t in range(TILES)]
        unit_t = keep.tile([P, TILES], F32, name="unit_t")
        wraw = {}
        for o in range(PASSES):
            for c in range(2):
                wraw[0, o, c] = keep.tile([P, PACK, WCOLS], F32, name="w1raw%d%d" % (o, c), align_bytes=64)[:]
                wraw[1, o, c] = keep.tile([P, PACK, WCOLS], F32, name="w2raw%d%d" % (o, c), tag=("kwin1", "kwin3", "kwin2", "bounded")[2 * o + c], align_bytes=64)[:]
        w3raw = keep.tile([P, PACK, N], F32, name="w3raw", align_bytes=64)

        nc.gpsimd.memset(xs[:].bitcast(I32), 0)

        def load_w(m, o, c):
            rows = (w1, w2)[m][o * P * PACK : (o + 1) * P * PACK, c * WCOLS : (c + 1) * WCOLS]
            nc.sync.dma_start(out=wraw[m, o, c], in_=rows.rearrange("(p j) c -> p j c", j=PACK))

        def load_x(o):
            nc.sync.dma_start(out=xw[o][:].bitcast(I32), in_=x_words[o].rearrange("p n t -> p (n t)").bitcast(I32))

        def load_q(t):
            nc.sync.dma_start(out=q[t][:], in_=qry[t * P : (t + 1) * P, :])

        nc.sync.dma_start(offs_t[:], offs)
        load_q(0)
        for quad in range(4):
            nc.sync.dma_start(out=xs[32 * quad : 32 * quad + 8, :].bitcast(I32), in_=x_scales[:, 4 * quad : 4 * quad + 4, :].bitcast(I32))
        load_x(0)
        load_w(0, 0, 0)
        load_x(1)
        load_w(0, 1, 0)
        for offsets, source in zip(lists, (b1, b2, b3)):
            nc.sync.dma_start(offsets[:], source)
        for o in range(PASSES):
            load_w(0, o, 1)
        for c in range(2):
            for o in range(PASSES):
                load_w(1, o, c)
        load_q(1)
        with nc.allow_non_contiguous_dma(reason="one value of unit a partition"):
            nc.sync.dma_start(out=unit_t[:], in_=unit.rearrange("(t p) o -> p (t o)", p=P))
        load_q(2)
        load_q(3)
        nc.sync.dma_start(out=w3raw[:], in_=w3.rearrange("(p j) c -> p j c", j=PACK))

        def open_key_window(t):
            kwin[t] = keep.tile([P, WINDOW], F32, name="kwin%d" % t, tag="kwin%d" % t, align_bytes=64)
            nc.gpsimd.memset(kwin[t][:, V:], 0.0)

        open_key_window(0)
        make_identity(nc, ident[:])
        for t in range(TILES):
            nc.gpsimd.memset(vwin[t][:, V:], 0.0)

        gs = keep.tile([P, S], U8, name="gs", align_bytes=64)
        ds = keep.tile([P, D, V], U8, name="ds", align_bytes=64)
        gw = {}
        dw = [keep.tile([P, D, V], U32, name="dw%d" % o, align_bytes=64) for o in range(PASSES)]

        def gather_words(o):
            gw[o] = keep.tile([P, S], U32, name="gw%d" % o, tag=("gw0", "wgroup000")[o], align_bytes=64)
            nc.vector.tensor_copy(gw[o][:], xw[o][:].indirect(offs_t[:]))

        def deal_words(o):
            nc.vector.tensor_copy(
                out=dw[o][:].rearrange("p d (a i) -> p a d i", i=4),
                in_=gw[o][:].rearrange("p (a i d) -> p a d i", i=4, d=D),
            )

        wq, wsc = {}, {}

        def cast_w(m, o, c):
            g = keep.tile([P, WCOLS, PACK], BF16, name="wgroup%d%d%d" % (m, o, c), tag="wgroup%d%d%d" % (m, o, c), align_bytes=64)
            nc.scalar.copy(out=g[:].rearrange("p (a i) j -> p a j i", i=4), in_=wraw[m, o, c].rearrange("p j (a i) -> p a j i", i=4))
            return g

        def quant_w(m, o, c, g):
            wq[m, o, c] = keep.tile([P, WCOLS], U32, name="wq%d%d%d" % (m, o, c), align_bytes=64)
            wsc[m, o, c] = keep.tile([P, WCOLS], U8, name="wsc%d%d%d" % (m, o, c), align_bytes=64)
            nc.vector.quantize_mx(out=wq[m, o, c][:].bitcast(FP8X4), scales=wsc[m, o, c][:], in_=g[:].rearrange("p c j -> p (c j)"))

        def product(m, t):
            acc = bank((0, 1, 6, 7)[t], [P, V], "acc%d%d" % (m, t))
            c, cols = t // 2, slice((t % 2) * P, (t % 2 + 1) * P)
            for o in range(PASSES):
                for d in range(D):
                    nc.tensor.matmul_mx(
                        out=acc[:],
                        lhsT=wq[m, o, c][:, cols].bitcast(FP8X4),
                        lhsT_scale=wsc[m, o, c][:, cols],
                        rhs=dw[o][:, d, :].bitcast(FP8X4),
                        rhs_scale=ds[4 * o : P, d, :],
                        start=(o == 0 and d == 0),
                        stop=(o == PASSES - 1 and d == D - 1),
                    )
            return acc

        nc.vector.tensor_copy(gs[:], xs[:].indirect(offs_t[:]))
        nc.vector.tensor_copy(out=ds[:].rearrange("p d (a i) -> p a d i", i=16), in_=gs[:].rearrange("p (a i d) -> p a d i", i=16, d=D))
        gather_words(0)
        quant_w(0, 0, 0, cast_w(0, 0, 0))
        deal_words(0)
        gather_words(1)
        quant_w(0, 1, 0, cast_w(0, 1, 0))
        deal_words(1)
        for o in range(PASSES):
            quant_w(0, o, 1, cast_w(0, o, 1))

        e = [keep.tile([P, LISTS, U], F32, name="e%d" % t, align_bytes=64) for t in range(TILES)]
        den, args = [], []

        def keys(t):
            a = keep.tile([P, LISTS, U], F32, name="arg%d" % t, tag=("wgroup011", "arg1", "wgroup110", "wgroup111")[t], align_bytes=64)
            for l in range(LISTS):
                nc.vector.tensor_tensor(a[:, l, :], kwin[t][:].indirect(lists[l][:]), q[t][:], MULT)
            for l in range(LISTS):
                nc.scalar.activation(th[:, l, :], a[:, l, :], ACT.Tanh, scale=1.0 / D)
            for l in range(LISTS):
                nc.scalar.activation(e[t][:, l, :], th[:, l, :], ACT.Exp)
            dsum = bank(2 + t, [P, U // P, P], "den%d" % t)
            for rb in range(U // P):
                for l in range(LISTS):
                    nc.tensor.matmul(dsum[:, rb, :], lhsT=e[t][:, l, rb * P : (rb + 1) * P], rhs=ident[:], is_transpose=True, start=(l == 0), stop=(l == LISTS - 1))
            den.append(dsum)
            args.append(a)

        def key_window(t):
            open_key_window(t)
            nc.scalar.copy(out=kwin[t][:, :V], in_=key[t][:])

        def val_window(t, acc):
            nc.scalar.activation(vwin[t][:, :V], acc[:], ACT.Copy, scale=unit_t[:, t : t + 1])

        key = [product(0, 0), product(0, 1)]
        nc.vector.tensor_copy(out=kwin[0][:, :V], in_=key[0][:])
        key.extend([product(0, 2), product(0, 3)])
        for n, (o, c) in enumerate(((0, 0), (1, 0), (0, 1), (1, 1))):
            quant_w(1, o, c, cast_w(1, o, c))
            if n + 1 < TILES:
                key_window(n + 1)
        val = [product(1, t) for t in range(TILES)]
        th = keep.tile([P, LISTS, U], F32, name="th", tag="bounded", align_bytes=64)
        keys(0)
        keys(1)
        val_window(0, val[0])
        val_window(1, val[1])
        keys(2)
        val_window(2, val[2])
        val_window(3, val[3])
        keys(3)

        logden = keep.tile([P, 2, TILES, HALF], F32, name="logden", tag="bounded", align_bytes=64)
        for t in range(TILES):
            nc.scalar.activation(logden[:, :, t, :], den[t][:].rearrange("p (h b) f -> p h (b f)", h=2), ACT.Ln, scale=float(D))
        recip = [keep.tile([P, 2, TILES, P], F32, name="recip%d" % h, tag="recip%d" % h, align_bytes=64) for h in range(2)]
        for h in range(2):
            nc.scalar.activation(recip[h][:].rearrange("r u t (g e) -> r u (t g) e", e=2), logden[:, h, :, :].rearrange("r t (g u e) -> r u (t g) e", u=2, e=2), ACT.Exp, scale=-1.0)

        w3g = keep.tile([P, N, PACK], BF16, name="w3g", tag="w3g", align_bytes=64)
        nc.scalar.copy(out=w3g[:].rearrange("p (a i) j -> p a j i", i=4), in_=w3raw[:].rearrange("p j (a i) -> p a j i", i=4))
        last = TILES - 1
        terms = keep.tile([P, TILES, LISTS, U], F32, name="terms", tag="kwin3", align_bytes=64)
        hid_t = [keep.tile([P, 2, 2, TILES, 32, 2], BF16, name="hid_t%d" % h, align_bytes=64) for h in range(2)]

        def add_up(b, t, first, count):
            nsum = bank(b, [P, count, P], "num%d%d" % (t, first))
            for rb in range(count):
                for l in range(LISTS):
                    cols = slice((first + rb) * P, (first + rb + 1) * P)
                    nc.tensor.matmul(nsum[:, rb, :], lhsT=terms[:, t, l, cols], rhs=ident[:], is_transpose=True, start=(l == 0), stop=(l == LISTS - 1))
            return nsum

        def normalise(nsum, h, t):
            nc.vector.tensor_tensor(
                hid_t[h][:, :, :, t, :, :],
                nsum.rearrange("r b (g u e) -> r u b g e", u=2, e=2),
                recip[h][:, :, t, :].rearrange("r u (b g e) -> r u b g e", b=2, e=2),
                MULT,
            )

        def project(h, blocks, back_bank, res_bank, queue):
            count = blocks.stop - blocks.start
            width = count * P
            first = h * HALF + blocks.start * P
            words = hid_t[h][:].rearrange("r u b t g e -> r u b (t g e)").bitcast(F32)
            back = bank(back_bank, [P, 2, count, P], "back%d" % first)
            for rb in range(count):
                for u in range(2):
                    nc.tensor.transpose(back[:, u, rb, :], words[:, u, blocks.start + rb, :], ident[:])
            hid = keep.tile([P, width * PACK], BF16, name="hid%d" % first, align_bytes=64)
            nc.scalar.copy(out=hid[:].bitcast(F32).rearrange("p (r u) -> p r u", u=2), in_=back[:].rearrange("p u b r -> p (b r) u"))
            hq = keep.tile([P, width], U32, name="hq%d" % first, align_bytes=64)
            hs = keep.tile([P, width], U8, name="hs%d" % first, align_bytes=64)
            nc.vector.quantize_mx(out=hq[:].bitcast(FP8X4), scales=hs[:], in_=hid[:])
            res = bank(res_bank, [P, width], "res%d" % first)
            nc.tensor.matmul_mx(out=res[:], lhsT=w3q[:].bitcast(FP8X4), lhsT_scale=w3s[:], rhs=hq[:].bitcast(FP8X4), rhs_scale=hs[:], start=True, stop=True)
            staged = keep.tile([P, width], F32, name="staged%d" % first, align_bytes=64)
            nc.scalar.copy(out=staged[:], in_=res[:])
            queue.dma_start(out=out[:, first : first + width], in_=staged[:])

        num = {}
        for t in range(TILES):
            for l in range(LISTS):
                nc.vector.tensor_tensor(terms[:, t, l, :], vwin[t][:].indirect(lists[l][:]), e[t][:, l, :], MULT)
            if t < last:
                nsum = add_up((0, 2, 3)[t], t, 0, 4)
                num[0, t], num[1, t] = nsum[:, 0:2, :], nsum[:, 2:4, :]
            else:
                num[0, t], num[1, t] = add_up(4, t, 0, 2)[:], add_up(5, t, 2, 2)[:]
        for h in range(2):
            for t in range(TILES):
                normalise(num[h, t], h, t)
        w3q = keep.tile([P, N], U32, name="w3q", align_bytes=64)
        w3s = keep.tile([P, N], U8, name="w3s", align_bytes=64)
        nc.vector.quantize_mx(out=w3q[:].bitcast(FP8X4), scales=w3s[:], in_=w3g[:].rearrange("p c j -> p (c j)"))
        project(0, slice(0, 2), 6, 1, nc.sync)
        for rb in range(2):
            project(1, slice(rb, rb + 1), (7, 4)[rb], (0, 2)[rb], (nc.sync, nc.scalar)[rb])
